import numpy as np
import ml_dtypes


def mxq(x, axis, fmt="e4m3"):
    dtype, down = {"e4m3": (ml_dtypes.float8_e4m3fn, 7), "e5m2": (ml_dtypes.float8_e5m2, 14)}[fmt]
    v = np.moveaxis(np.asarray(x, np.float32).astype(ml_dtypes.bfloat16).astype(np.float64), axis, -1)
    blocks = v.reshape(v.shape[:-1] + (-1, 32))
    amax = np.abs(blocks).max(-1, keepdims=True)
    byte = np.maximum(np.where(amax > 0, np.frexp(amax)[1] - 1 + 127, 0) - down, 1)
    scale = np.exp2(byte - 127.0)
    codes = (blocks / scale).astype(np.float32).astype(dtype).astype(np.float64)
    return np.moveaxis((codes * scale).reshape(v.shape), -1, axis)


WIDE = False


def mx_kscale(k):
    if not WIDE:
        return np.ones(k)
    levels = np.array([10, -10, 5, -5, 0])
    if k % 512:
        return np.exp2(np.random.permutation(np.resize(levels, k // 32))).repeat(32)
    a = np.empty((k // 512, 16))
    for p in range(k // 512):
        a[p, :8] = np.random.permutation(np.resize(levels, 8))
        for g in range(8):
            far = levels[np.abs(levels - a[p, g]) >= 10]
            a[p, g + 8] = far[np.random.randint(len(far))]
    return np.exp2(a.ravel()).repeat(32)


BF16 = ml_dtypes.bfloat16


def bf(x):
    return np.asarray(x, np.float32).astype(BF16)


def f64(x):
    return np.asarray(x).astype(np.float64)

def planes(Y):
    n, m = Y.shape
    b = f64(bf(Y)).reshape(n // 32, 32, m)
    amax = np.abs(b).max(1)
    byte = np.clip(np.where(amax > 0, np.frexp(amax)[1] - 1 + 127 - 7, 1), 1, 254)
    codes = (b * np.exp2(127.0 - byte)[:, None, :]).reshape(n, m).astype(np.float32).astype(ml_dtypes.float8_e4m3fn).view(np.uint8)
    words = codes.reshape(n // 512, 128, 4, m).transpose(0, 1, 3, 2)
    return np.ascontiguousarray(words), np.ascontiguousarray(byte.astype(np.uint8).reshape(n // 512, 16, m))


B, T, DK, DV = 3, 512, 512, 512

W_MASS = 512.0


def setup_inputs():
    s, t = mx_kscale(T), mx_kscale(DK)
    return {
        "q": bf(np.random.standard_normal((B, T, DK)) / np.sqrt(DK) / t),
        "k": bf(np.random.standard_normal((B, T, DK)) * 0.7 * s[:, None]),
        "v": bf(np.random.standard_normal((B, T, DV)) / np.sqrt(T) / s[:, None]),
        "eta": bf(np.random.uniform(0.5, 1.5, (B, T))),
        "logw": bf(np.random.standard_normal((B, DK, DV)) * 0.8),
        "alpha": bf(np.random.uniform(0.5, 0.95, DV)),
        "g": bf(np.random.standard_normal(DK) * t),
    }


def hebbian_write(k, v, eta):
    kw = k * eta[:, :, None]
    return mxq(kw, 1, "e4m3").transpose(0, 2, 1) @ mxq(v, 1, "e4m3")


def kl_retention(logw, h, alpha):
    l = alpha[None, None, :] * logw + h
    e = np.exp(l - l.max(axis=1, keepdims=True))
    return W_MASS * (e / e.sum(axis=1, keepdims=True))


def core(q, k, v, eta, logw, alpha, g):
    h = hebbian_write(f64(k), f64(v), f64(eta))
    w = kl_retention(f64(logw), h, f64(alpha))
    wg = f64(g)[None, :, None] * w
    return mxq(f64(q), 2, "e4m3") @ mxq(wg, 1, "e4m3")


def reference(q, k, v, eta, logw, alpha, g):
    R_out = core(q, k, v, eta, logw, alpha, g)
    words, scales = planes(np.moveaxis(R_out, 1, 0).reshape(512, -1))
    return R_out, words, scales

from contextlib import ExitStack

import concourse.mybir as mybir
from concourse.masks import make_identity

B, T, DK, DV = 3, 512, 512, 512
MASS = 512.0
FLOPS = 2 * 2 * B * T * DK * DV

F32 = mybir.dt.float32
BF16 = mybir.dt.bfloat16
U32 = mybir.dt.uint32
I32 = mybir.dt.int32
U8 = mybir.dt.uint8
FP8X4 = mybir.dt.float8_e4m3fn_x4
ALU = mybir.AluOpType
AF = mybir.ActivationFunctionType
AX = mybir.AxisListType

P = 128
PER = DV // P
GROUPS = [[0, 1], [2, 3], [4, 5], [6, 7], [8, 9], [10], [11]]

SCHEDULE = """
    scale_k.v:0:0 scale_k.s:0:3 spread_gain scale_k.v:0:1 scale_k.v:0:2 turn_alpha weave_v.v:0:0:128
    weave_v.s:0:128:256 weave_k.v:0:0:128 turn_logw:0 copy_gain quant_v:0:0:128 weave_k.v:0:128:256
    weave_v.s:0:256:384 quant_v:0:128:256 weave_v.v:0:384:512 turn_logw:1 copy_logw.v:0 weave_k.s:0:384:512
    quant_v:0:256:384 quant_v:0:384:512 copy_alpha weave_k.v:0:256:384 copy_logw.s:1 turn_q:0 quant_k:0
    scale_k.v:1:0 scale_k.s:1:1 scale_k.v:1:2 write:0 scale_k.v:1:3 copy_q.v:0:0 copy_q.s:0:1 write:1
    weave_k.g:1:0:256 weave_v.s:1:0:256 decay:0 decay:1 write:2 top:0:1 weave_k.g:1:256:512
    weave_v.s:1:256:512 turn_logw:2 top:1:2 write:3 decay:2 turn_logw:3 exp:0 quant_q:0 exp:1 turn_q:1
    quant_k:1 copy_logw.s:2 quant_v:1:0:512 copy_logw.s:3 invert:0 scale_k.v:2:0 decay:3 scale_k.s:2:1
    write:4 gate:0 scale_k.s:2:2 write:5 gate:1 scale_k.s:2:3 turn_logw:4 top:2:4 copy_q.s:1:0
    weave_k.g:2:0:256 copy_q.s:1:1 turn_logw:5 decay:4 copy_logw.s:4 decay:5 turn_q:2 exp:2
    weave_k.g:2:256:512 top:4:5 exp:3 top:5:6 write:6 copy_logw.s:5 quant_q:1 write:7 exp:4 invert:1
    turn_w:0 quant_k:2 exp:5 turn_w:1 gate:2 weave_v.s:2:0:256 gate:3 invert:2 decay:6 copy_w.s:0 gate:4
    weave_v.s:2:256:512 top:6:7 turn_w:2 turn_w:3 quant_w:0 gate:5 exp:6 read:1 quant_v:2:0:512 copy_w.s:1
    read:0 decay:7 copy_q.s:2:0 write:8 quant_w:1 turn_w:4 result.s:0 top:7:8 write:9 result.s:1 decay:8
    read:3 pack.g:0 read:2 exp:7 decay:9 turn_w:5 store_result:0 pack.g:1 result.s:3 write:10 top:8:9
    write:11 copy_w.s:2 top:9:10 exp:8 quant_out:0 invert:3 quant_w:2 exp:9 gate:6 store_words:0 read:5
    result.s:2 gate:7 read:4 copy_q.s:2:1 invert:4 turn_w:6 decay:10 pack.g:2 store_result:1 turn_w:7
    result.s:4 decay:11 copy_w.s:3 pack.g:3 top:10:11 result.s:5 top:11:12 exp:10 gate:8 store_result:2
    exp:11 gate:9 turn_w:8 pack_bank.s:4 quant_out:1 quant_w:3 turn_w:9 pack_bank.s:5 invert:5 quant_q:2
    store_words:1 store_scales:0 read:7 copy_w.s:4 gate:10 read:6 gate:11 result.s:7 turn_w:10 quant_out:2
    pack_bank.s:6 quant_w:4 turn_w:11 result.v:6 copy_w.s:5 store_words:2 pack_bank.s:7 read:9 quant_w:5
    copy_w.s:6 store_result:3 read:8 quant_out:3 read:10 result.s:8 result.v:9 store_words:3 store_scales:1
    quant_w:6 result.s:10 pack_bank.v:8 store_result:4 read:11 pack.v:9 pack.g:10 store_result:5 result.s:11
    quant_out:4 quant_out:5 store_result:6 pack.v:11 store_words:4 store_words:5 quant_out:6 store_words:6
    store_scales:2
"""


def tile_klretentionhebbianmemorywriteread_x1_kernel(
    tc, q, k, v, eta, logw, alpha, g, out_0, out_1, out_2
):
    nc = tc.nc

    with ExitStack() as ctx:
        once = ctx.enter_context(tc.tile_pool(name="once", bufs=1))
        raw = ctx.enter_context(tc.tile_pool(name="raw", bufs=B))
        two = ctx.enter_context(tc.tile_pool(name="two", bufs=2))
        three = ctx.enter_context(tc.tile_pool(name="three", bufs=3))
        four = ctx.enter_context(tc.tile_pool(name="four", bufs=4))
        ps_write = ctx.enter_context(tc.psum_pool(name="ps_write", bufs=2))
        ps_turn = ctx.enter_context(tc.psum_pool(name="ps_turn", bufs=3))
        ps_read = ctx.enter_context(tc.psum_pool(name="ps_read", bufs=3))
        ctx.enter_context(tc.manual_schedule())

        made = {}

        eta_rows = once.tile([P, T], BF16, name="eta_rows")
        nc.gpsimd.memset(eta_rows[:].bitcast(I32), 0)
        rows = once.tile([P, DK], BF16, name="rows")
        nc.gpsimd.memset(rows[:].bitcast(I32), 0)
        ident_bf16 = once.tile([P, P], BF16, name="ident_bf16")
        make_identity(nc, ident_bf16[:])
        ident_f32 = once.tile([P, P], F32, name="ident_f32")
        make_identity(nc, ident_f32[:])

        first_row = once.tile([P, P], BF16, name="first_row")
        nc.vector.memset(first_row[:], 0.0)
        nc.scalar.activation(first_row[0:1, :], first_row[0:1, :], AF.Exp)

        for n in range(B):
            nc.sync.dma_start(out=eta_rows[n : n + 1, :], in_=eta[n : n + 1, :])
        k_raw, v_raw, logw_raw, q_raw = [], [], [], []
        for n in range(B):
            k_tile = raw.tile([P, 4, DK], BF16, name="k_tile")
            v_tile = raw.tile([P, 4, DV], BF16, name="v_tile")
            logw_tile = raw.tile([P, 4, DV], BF16, name="logw_tile")
            q_tile = raw.tile([P, 4, DK], BF16, name="q_tile")
            pieces = 2 if n == 0 else 1
            k_n = k[n].rearrange("(p j) w -> p j w", j=4)
            v_n = v[n].rearrange("(p j) w -> p j w", j=4)
            logw_n = logw[n].rearrange("(b p) w -> p b w", p=P)
            for i in range(pieces):
                js = slice(i * 4 // pieces, (i + 1) * 4 // pieces)
                nc.sync.dma_start(out=k_tile[:, js, :], in_=k_n[:, js, :])
            if n == 0:
                nc.sync.dma_start(out=rows[0:1, :], in_=g.unsqueeze(0))
                nc.sync.dma_start(out=rows[1:2, :], in_=alpha.unsqueeze(0))
            for i in range(pieces):
                cs = slice(i * DV // pieces, (i + 1) * DV // pieces)
                nc.sync.dma_start(out=v_tile[:, :, cs], in_=v_n[:, :, cs])
                nc.sync.dma_start(out=logw_tile[:, :, cs], in_=logw_n[:, :, cs])
            nc.sync.dma_start(out=q_tile[:], in_=q[n].rearrange("(p i) w -> p i w", i=4))
            k_raw.append(k_tile)
            v_raw.append(v_tile)
            logw_raw.append(logw_tile)
            q_raw.append(q_tile)

        turned = ps_turn.tile([P, 4, P], BF16, name="turned")
        for j in range(4):
            nc.tensor.transpose(turned[:, j, :], eta_rows[:, j:T:4], ident_bf16[:])
        eta_col = once.tile([P, B, 4], F32, name="eta_col")
        nc.vector.tensor_copy(out=eta_col[:], in_=turned[:, :, 0:B].rearrange("p j n -> p n j"))

        def copy(engine, out, in_):
            if engine == "s":
                nc.scalar.copy(out, in_)
            elif engine == "v":
                nc.vector.tensor_copy(out=out, in_=in_)
            else:
                nc.gpsimd.tensor_scalar(out=out, in0=in_, scalar1=1.0, scalar2=0.0, op0=ALU.mult, op1=ALU.add)

        def columns(s):
            return slice(s % PER * P, (s % PER + 1) * P)

        def group_of(s):
            for gi, chunks in enumerate(GROUPS):
                if s in chunks:
                    return gi, chunks.index(s)

        def words(ap):
            return ap.rearrange("p w j -> p (w j)").bitcast(F32)

        def turn_alpha():
            made["alpha_psum"] = ps_turn.tile([P, PER, P], BF16, name="turned")
            for c in range(PER):
                nc.tensor.transpose(made["alpha_psum"][:, c, :], rows[:, c * P : (c + 1) * P], ident_bf16[:])

        def copy_alpha():
            made["alpha"] = once.tile([P, PER, 1], F32, name="alpha_col")
            nc.scalar.copy(made["alpha"][:], made["alpha_psum"][:, :, 1:2])

        def spread_gain():
            made["gain_psum"] = ps_turn.tile([P, DK], F32, name="turned")
            nc.tensor.matmul(
                made["gain_psum"][:],
                lhsT=first_row[:],
                rhs=rows[:].rearrange("p (m u b) -> p u m b", u=2, b=2),
                start=True,
                stop=True,
            )

        def copy_gain():
            made["gain"] = once.tile([P, DK], F32, name="gain", align_bytes=64)
            nc.scalar.activation(made["gain"][:], made["gain_psum"][:], AF.Copy, scale=MASS)

        def scale_k(engine, n, j):
            if ("k_scaled", n) not in made:
                made["k_scaled", n] = two.tile([P, 4, DK], BF16, name="k_scaled", align_bytes=64)
            out, in_, factor = made["k_scaled", n][:, j, :], k_raw[n][:, j, :], eta_col[:, n, j : j + 1]
            if engine == "s":
                nc.scalar.activation(out, in_, AF.Copy, scale=factor)
            else:
                nc.vector.tensor_scalar(out=out, in0=in_, scalar1=factor, scalar2=None, op0=ALU.mult)

        def weave(engine, what, n, source, c0, c1):
            if (what, n) not in made:
                made[what, n] = two.tile([P, 512, 4], BF16, name=what, align_bytes=64)
            out = made[what, n][:, c0:c1, :]
            in_ = source[:, :, c0:c1]
            if engine == "g":
                copy(engine, out, in_.rearrange("p j w -> p w j"))
            else:
                copy(
                    engine,
                    out.rearrange("p (w i) j -> p w j i", i=4),
                    in_.rearrange("p j (w i) -> p w j i", i=4),
                )

        def weave_k(engine, n, c0, c1):
            weave(engine, "k_woven", n, made["k_scaled", n], c0, c1)

        def weave_v(engine, n, c0, c1):
            weave(engine, "v_woven", n, v_raw[n], c0, c1)

        def quantise(codes, scales, source):
            nc.vector.quantize_mx(
                out=codes.bitcast(FP8X4), scales=scales, in_=source.rearrange("p w j -> p (w j)")
            )

        def quant_operand(what, n, source, c0, c1):
            if (what, n) not in made:
                codes = two.tile([P, 512], U32, name=what + "_codes", align_bytes=64)
                scales = two.tile([P, 512], U8, name=what + "_scales", align_bytes=64)
                made[what, n] = codes, scales
            codes, scales = made[what, n]
            quantise(codes[:, c0:c1], scales[:, c0:c1], source[:, c0:c1, :])

        def quant_k(n):
            quant_operand("k", n, made["k_woven", n], 0, DK)

        def quant_v(n, c0, c1):
            quant_operand("v", n, made["v_woven", n], c0, c1)

        def turn_q(n):
            q_words = q_raw[n][:].rearrange("p i k -> p (i k)").bitcast(F32)
            for half in range(2):
                turned = ps_turn.tile([P, 2, 2, P], F32, name="turned")
                for a in range(2):
                    i = 2 * half + a
                    for u in range(2):
                        nc.tensor.transpose(
                            turned[:, a, u, :], q_words[:, 256 * i + u : 256 * (i + 1) : 2], ident_f32[:]
                        )
                made["q_psum", n, half] = turned

        def copy_q(engine, n, half):
            if ("q_woven", n) not in made:
                made["q_woven", n] = two.tile([P, T, 4], BF16, name="q_woven", align_bytes=64)
            copy(
                engine,
                words(made["q_woven", n][:, 256 * half : 256 * (half + 1), :]).rearrange(
                    "p (a m u) -> p a m u", a=2, u=2
                ),
                made["q_psum", n, half][:].rearrange("p a u m -> p a m u"),
            )

        def quant_q(n):
            quant_operand("q", n, made["q_woven", n], 0, T)

        def turn_logw(pair):
            n, c = divmod(2 * pair, PER)
            turned = ps_turn.tile([P, 2, 4, P], BF16, name="turned")
            for a in range(2):
                for b in range(4):
                    nc.tensor.transpose(
                        turned[:, a, b, :], logw_raw[n][:, b, (c + a) * P : (c + a + 1) * P], ident_bf16[:]
                    )
            made["logw_psum", pair] = turned

        def copy_logw(engine, pair):
            made["logw", pair] = three.tile([P, 2, DK], BF16, name="logw_turned", align_bytes=64)
            copy(
                engine,
                made["logw", pair][:].rearrange("p a k -> p (a k)").bitcast(F32),
                made["logw_psum", pair][:].rearrange("p a b m -> p (a b m)").bitcast(F32),
            )

        def write(s):
            n = s // PER
            made["h", s] = ps_write.tile([P, DK], F32, name="h")
            v_codes, v_scales = made["v", n]
            k_codes, k_scales = made["k", n]
            nc.tensor.matmul_mx(
                made["h", s][:],
                lhsT=v_codes[:, columns(s)].bitcast(FP8X4),
                lhsT_scale=v_scales[:, columns(s)],
                rhs=k_codes[:].bitcast(FP8X4),
                rhs_scale=k_scales[:],
                start=True,
                stop=True,
            )

        def decay(s):
            pair, a = divmod(s, 2)
            if ("l", pair) not in made:
                made["l", pair] = three.tile([P, 2, DK], F32, name="l", align_bytes=64)
                made["minus_top", pair] = three.tile([P, 2], F32, name="minus_top", align_bytes=64)
            nc.vector.scalar_tensor_tensor(
                out=made["l", pair][:, a, :],
                in0=made["logw", pair][:, a, :],
                scalar=made["alpha"][:, s % PER, 0:1],
                in1=made["h", s][:],
                op0=ALU.mult,
                op1=ALU.add,
            )

        def top(s0, s1):
            pair, a = divmod(s0, 2)
            chunks = slice(a, a + s1 - s0)
            nc.vector.tensor_reduce(
                out=made["minus_top", pair][:, chunks],
                in_=made["l", pair][:, chunks, :],
                axis=AX.X,
                op=ALU.max,
                negate=True,
            )

        def exp(s):
            pair, a = divmod(s, 2)
            made["e", s] = four.tile([P, DK], F32, name="e", align_bytes=64)
            if ("total", pair) not in made:
                made["total", pair] = three.tile([P, 2], F32, name="total", align_bytes=64)
            nc.scalar.activation(
                made["e", s][:].rearrange("p (u m b) -> p u m b", u=2, b=2),
                made["l", pair][:, a, :].rearrange("p (m u b) -> p u m b", u=2, b=2),
                AF.Exp,
                bias=made["minus_top", pair][:, a : a + 1],
                accum_out=made["total", pair][:, a : a + 1],
            )

        def invert(pair):
            made["inverse", pair] = three.tile([P, 2], F32, name="inverse", align_bytes=64)
            nc.vector.reciprocal(made["inverse", pair][:], made["total", pair][:])

        def gate(s):
            pair, a = divmod(s, 2)
            made["wg", s] = three.tile([P, DK], BF16, name="wg", align_bytes=64)
            nc.vector.scalar_tensor_tensor(
                out=made["wg", s][:],
                in0=made["e", s][:],
                scalar=made["inverse", pair][:, a : a + 1],
                in1=made["gain"][:],
                op0=ALU.mult,
                op1=ALU.mult,
            )

        def turn_w(s):
            gi, a = group_of(s)
            if ("wg_psum", gi) not in made:
                made["wg_psum", gi] = ps_turn.tile([P, len(GROUPS[gi]), 2, P], F32, name="turned")
            wg_words = made["wg", s][:].bitcast(F32)
            for u in range(2):
                nc.tensor.transpose(
                    made["wg_psum", gi][:, a, u, :], wg_words[:, u * P : (u + 1) * P], ident_f32[:]
                )

        def copy_w(engine, gi):
            count = len(GROUPS[gi])
            made["wg_woven", gi] = two.tile([P, 2 * P, 4], BF16, name="wg_woven", align_bytes=64)
            copy(
                engine,
                words(made["wg_woven", gi][:, 0 : count * P, :]).rearrange("p (a m u) -> p a m u", a=count, u=2),
                made["wg_psum", gi][:].rearrange("p a u m -> p a m u"),
            )

        def quant_w(gi):
            width = len(GROUPS[gi]) * P
            codes = two.tile([P, 2 * P], U32, name="wg_codes", align_bytes=64)
            scales = two.tile([P, 2 * P], U8, name="wg_scales", align_bytes=64)
            quantise(codes[:, 0:width], scales[:, 0:width], made["wg_woven", gi][:, 0:width, :])
            made["wg_quant", gi] = codes, scales

        def read(s):
            gi, a = group_of(s)
            q_codes, q_scales = made["q", s // PER]
            w_codes, w_scales = made["wg_quant", gi]
            place = slice(a * P, (a + 1) * P)
            made["out_psum", s] = ps_read.tile([P, 4, P], F32, name="out_psum")
            for i in range(4):
                times = slice(i * P, (i + 1) * P)
                nc.tensor.matmul_mx(
                    made["out_psum", s][:, i, :],
                    lhsT=q_codes[:, times].bitcast(FP8X4),
                    lhsT_scale=q_scales[:, times],
                    rhs=w_codes[:, place].bitcast(FP8X4),
                    rhs_scale=w_scales[:, place],
                    start=True,
                    stop=True,
                )

        def result(engine, s):
            n = s // PER
            if ("out", n) not in made:
                made["out", n] = two.tile([P, 4, DV], F32, name="out_tile", align_bytes=64)
            copy(engine, made["out", n][:, :, columns(s)], made["out_psum", s][:])

        def pack_from(engine, s, source):
            gi, a = group_of(s)
            if ("out_woven", gi) not in made:
                made["out_woven", gi] = two.tile([P, 2 * P, 4], BF16, name="out_woven", align_bytes=64)
            copy(engine, made["out_woven", gi][:, a * P : (a + 1) * P, :], source.rearrange("p i m -> p m i"))

        def pack(engine, s):
            pack_from(engine, s, made["out", s // PER][:, :, columns(s)])

        def pack_bank(engine, s):
            pack_from(engine, s, made["out_psum", s][:])

        def place_of(gi):
            n, c = divmod(GROUPS[gi][0], PER)
            return n, slice(c * P, (c + len(GROUPS[gi])) * P)

        def quant_out(gi):
            n, cs = place_of(gi)
            if ("planes", n) not in made:
                codes = three.tile([P, DV], U32, name="out_codes", align_bytes=64)
                scales = three.tile([P, DV], U8, name="out_scales", align_bytes=64)
                made["planes", n] = codes, scales
            codes, scales = made["planes", n]
            quantise(codes[:, cs], scales[:, cs], made["out_woven", gi][:, 0 : len(GROUPS[gi]) * P, :])

        def store_result(gi):
            n, cs = place_of(gi)
            nc.sync.dma_start(
                out=out_0[n].rearrange("(p i) m -> p i m", i=4)[:, :, cs], in_=made["out", n][:, :, cs]
            )

        def store_words(gi):
            n, cs = place_of(gi)
            nc.sync.dma_start(
                out=out_1[0].rearrange("p m t -> p (m t)").bitcast(I32)[:, n * DV + cs.start : n * DV + cs.stop],
                in_=made["planes", n][0][:, cs].bitcast(I32),
            )

        def store_scales(n):
            width = DV // 4
            for r in range(4):
                nc.sync.dma_start(
                    out=out_2[0].bitcast(I32)[4 * r : 4 * r + 4, n * width : (n + 1) * width],
                    in_=made["planes", n][1][32 * r : 32 * r + 4, :].bitcast(I32),
                )

        stages = {
            "turn_alpha": turn_alpha,
            "copy_alpha": copy_alpha,
            "spread_gain": spread_gain,
            "copy_gain": copy_gain,
            "scale_k": scale_k,
            "weave_k": weave_k,
            "weave_v": weave_v,
            "quant_k": quant_k,
            "quant_v": quant_v,
            "turn_q": turn_q,
            "copy_q": copy_q,
            "quant_q": quant_q,
            "turn_logw": turn_logw,
            "copy_logw": copy_logw,
            "write": write,
            "decay": decay,
            "top": top,
            "exp": exp,
            "invert": invert,
            "gate": gate,
            "turn_w": turn_w,
            "copy_w": copy_w,
            "quant_w": quant_w,
            "read": read,
            "result": result,
            "pack": pack,
            "pack_bank": pack_bank,
            "quant_out": quant_out,
            "store_result": store_result,
            "store_words": store_words,
            "store_scales": store_scales,
        }
        for token in SCHEDULE.split():
            numbers = token.split(":")
            engine = numbers[0].split(".")
            stages[engine[0]](*engine[1:], *[int(x) for x in numbers[1:]])
